import numpy as np, ml_dtypes
CORES = [13,21,141,149]
N = 4
BF = ml_dtypes.bfloat16
W, T, FC, SC, HB, RO, NB, LN = 2048, 256, 512, 256, 2048, 3, 2, 64
def pick(tab, ix):
    return np.take_along_axis(tab, ix[:, :, None, :], 3)
def hashes(hw, z):
    return np.sum(hw * z, axis=-2) & (HB - 1)
def compose(a, b):
    return (((a * b) >> 5) + a + 37 * b) & (W - 1)
def parts(rng):
    x = rng.integers(0, 256, (N, 8, 16, W)); x[:, :, 15] = rng.integers(0, 16, (N, 8, W))
    fw = rng.integers(0, W, (N, 8, 16, FC)); sw = rng.integers(0, W, (N, 8, 16, SC)); aw = rng.integers(0, W, (N, 8, 16, SC))
    z = rng.integers(0, 256, (N, 8, 16, T)); z[:, :, 15] = 0
    q = rng.integers(0, W, (N, 8, T)); hw = rng.integers(1, 256, (N, 8, 16, 1)); hw[:, :, 15] = 0
    th = rng.integers(800, 1101, (N, 8, 1))
    return x, fw, sw, aw, z, q, hw, th
def pack(x, fw, sw, aw, z, q, hw, th):
    return {"lx": x.reshape(N, 128, W).astype(np.float32).astype(BF), "fw": fw.reshape(N, 128, FC).astype(np.int32), "sw": sw.reshape(N, 128, SC).astype(np.int32), "aw": aw.reshape(N, 128, SC).astype(np.int32),
            "z0": z.reshape(N, 128, T).astype(np.float32).astype(BF), "q0": q.astype(np.int32), "hw": hw.reshape(N, 128, 1).astype(np.int32), "th": th.astype(np.int32)}
def setup_inputs(rng):
    return pack(*parts(rng))
def setup_inputs_spread(rng):
    x, fw, sw, aw, z, q, hw, th = parts(rng)
    x[:, :, :15] = (np.exp2(8 * rng.random((N, 8, 1, W))) * rng.random((N, 8, 15, W))).astype(np.int64); x[:, :, 15] = (16 * rng.random((N, 8, W)) ** 2).astype(np.int64)
    z[:, :, :15] = (np.exp2(8 * rng.random((N, 8, 1, T))) * rng.random((N, 8, 15, T))).astype(np.int64)
    e = rng.choice(np.array([1.0, 2.0, 4.0]), (N, 8, 1, 1))
    fw, sw, aw = [np.minimum((W * rng.random(v.shape) ** e).astype(np.int64), W - 1) for v in (fw, sw, aw)]
    q = np.minimum((W * rng.random(q.shape) ** e[..., 0]).astype(np.int64), W - 1)
    hw[:, :, :15] = (np.exp2(8 * rng.random((N, 8, 15, 1))) * rng.random((N, 8, 15, 1))).astype(np.int64)
    th = rng.choice(np.array([150, 250, 400, 800, 1300, 2500, 4095]), (N, 8, 1))
    return pack(x, fw, sw, aw, z, q, hw, th)
def setup_inputs_ends(rng):
    def two(hi, *shape):
        return hi * rng.integers(0, 2, shape)
    x = two(255, N, 8, 16, W); k = rng.integers(0, 3, (N, 8, 1, W)); x = np.where(k == 0, x, np.where(k == 1, 0, 255)); x[:, :, 15] = two(15, N, 8, W)
    fw = two(W - 1, N, 8, 16, FC); sw = two(W - 1, N, 8, 16, SC); aw = two(W - 1, N, 8, 16, SC); sw[..., SC - 1] = W - 1; aw[..., SC - 1] = W - 1
    z = two(255, N, 8, 16, T); k = rng.integers(0, 3, (N, 8, 1, T)); z = np.where(k == 0, z, np.where(k == 1, 0, 255)); z[..., T - 1] = 255
    q = two(W - 1, N, 8, T); hw = two(255, N, 8, 16, 1); hw[:, 7] = 255; hw[:, 0, 0] = 0
    hw[:, 6] = 0; hw[:, 6, 0] = 255; hw[:, 6, 1] = 2; hw[:, :, 15] = 0
    th = np.full((N, 8, 1), 4095); used = np.array([0, W - 1, W - 37, compose(W - 1, W - 1)])
    for a in range(N):
        for g in range(8):
            m = (g + N - 1 - a) % 4
            if m == 0:
                x[a, g][:, 0] = 0; x[a, g][:15, W - 1] = 255; x[a, g, 15, W - 1] = 15
                if g < 4: th[a, g] = 0
            elif m == 2:
                x[a, g][:15, used] = 255; x[a, g][15, used] = 15
            elif m == 3:
                x[a, g][:, used] = 0; z[a, g][:, T // 2:] = 255
    z[:, :, 15] = 0
    return pack(x, fw, sw, aw, z, q, hw, th)
def setup_inputs_corners(rng):
    x, fw, sw, aw, z, q, hw, th = parts(rng); x[:, :, 15] = rng.choice(np.array([0, 1, 13, 14, 15]), (N, 8, W))
    for a in range(N):
        for g in range(8):
            m = (a + g) % 4
            if m == 0:
                v = rng.permutation(W)[:T]; d = rng.integers(99, 102, T); y = np.array(z[a, g]); y[0] = np.where(y[0] < 128, y[0] + d, y[0] - d); y[15] = 15
                x[a, g][:, v] = y; q[a, g] = v; th[a, g] = 100
            elif m == 1:
                h = hashes(hw[a, g], z[a, g]); fw[a, g][:, h >> 2] = compose(sw[a, g][:, h & (SC - 1)], aw[a, g][:, h >> 3]); th[a, g] = 4095
            elif m == 2:
                fw[a, g] = rng.choice(np.array([0, 1, W - 2, W - 1]), (16, FC)); q[a, g] = np.arange(T); hw[a, g, :15] = 255 * (a & 1); th[a, g] = 1200
            else:
                x[a, g][:15] = 128; th[a, g] = 1000
    return pack(x, fw, sw, aw, z, q, hw, th)
def setup_inputs_crowd(rng):
    x, fw, sw, aw, z, q, hw, th = parts(rng); mid = rng.integers(0, 80, (N, 8, 15, 1))
    for a in range(N):
        for g in range(8):
            t = int(rng.integers(0, T)); odd = np.array(z[a, g][:, t]); one = np.array(z[a, g][:, (t + 1) % T]); full = np.array(one); full[15] = 15
            if g == 4 or g == 5:
                to = (a + 1 + np.arange(T) // (T // NB)) % N; e = rng.multinomial(T - rng.integers(0, 3, T), np.full(15, 1.0 / 15)).T
                x[a, g][:15] = mid[a, g]; z[a, g][:15] = np.minimum(mid[a, g] + mid[:, g, :, 0][to].T + e, 255); th[a, g] = g - 4
                if g == 5: z[a, g][:15, t] = mid[a, g, :, 0]; x[a, g, 15, q[a, g, t]] = 15
            elif g == 7 and a & 1:
                hw[a, g] = 0; hw[a, g, 0] = 8; hw[a, g, 1] = 1; th[a, g] = 4095
                y = rng.integers(96, 160, (16, T)); y[0] = rng.permutation(256)[:T]; y[1] = rng.integers(0, 8, T); y[15] = 0; z[a, g] = y
                h = hashes(hw[a, g], y)[:LN]; cs = compose(sw[a, g][:, h & (SC - 1)], aw[a, g][:, h >> 3]); near = np.isin(np.arange(W), cs); rest = np.flatnonzero(~near)
                x[a, g][2:15] = np.where(near, rng.integers(96, 160, (13, W)), 255 * rng.integers(0, 2, (13, W))); x[a, g][15] = np.where(near, 15, 0)
                fw[a, g][:, h >> 2] = rng.choice(rest, (16, LN)); q[a, g, :LN] = rng.choice(rest, LN)
            elif g == 7:
                z[a, g] = z[a, g][:, np.arange(T) & 3]; th[a, g] = 4095
            else:
                z[a, g] = one[:, None]; h = int(hashes(hw[a, g], one[:, None])[0]); cs = compose(sw[a, g][:, h & (SC - 1)], aw[a, g][:, h >> 3])
                if g < 2:
                    v = int(rng.integers(0, W)); x[a, g][:, v] = full; q[a, g] = v; th[a, g] = 1
                elif g < 4:
                    v = int(cs[5]); o = (v + 1) & (W - 1); x[a, g][:, v] = full; q[a, g] = o; c = fw[a, g][:, h >> 2]; fw[a, g][:, h >> 2] = np.where(c == v, o, c); th[a, g] = 4095 if g == 2 else 1
                else:
                    p = rng.permutation(W); p = p[~np.isin(p, cs)][:T]; x[a, g][:, p] = full[:, None]; q[a, g] = p; fw[a, g][:, h >> 2] = cs; th[a, g] = 4095
                if g in (1, 3): z[a, g][:, t] = odd
    return pack(x, fw, sw, aw, z, q, hw, th)
def setup_inputs_ties(rng):
    x, fw, sw, aw, z, q, hw, th = parts(rng)
    x[:, :, :15] = rng.integers(100, 102, (N, 8, 15, W)); x[:, :, 15] = rng.integers(3, 5, (N, 8, W)); z[:, :, :15] = rng.integers(100, 102, (N, 8, 15, T)); th = rng.integers(178, 187, (N, 8, 1))
    x[:, 2::3, :15] = rng.integers(0, 4, (N, 2, 15, W)); x[:, 2::3, 15] = 0; th[:, 2::3] = rng.integers(3985, 4006, (N, 2, 1))
    less = (np.arange(T) & 7) == rng.integers(0, 8, (N, 2, 1, 1))
    z[:, 2::3, :15] = np.where(less, rng.integers(200, 256, (N, 2, 15, T)), rng.integers(254, 256, (N, 2, 15, T)))
    mid = rng.integers(140, 160, (N, 8, 15)); goal = 2049 + 2 * rng.integers(0, 4, (N, 8))
    for a in range(N):
        to = (a + 1 + np.arange(T) // (T // NB)) % N
        for g in (1, 6):
            n = (a + g // 3) % 4
            least = goal[to, g] + rng.integers(-2, 2, T)
            d = rng.multinomial(np.sum(mid[to, g], axis=1) - least, np.full(15, 1.0 / 15)).T
            x[a, g][:15] = mid[a, g][:, None]; x[a, g][15] = 15; z[a, g][:15] = np.minimum(mid[a, g][:, None] + d, 255)
            z[a, g][:, rng.permutation(T)[:n]] = 0; th[a, g] = goal[a, g] - n
    return pack(x, fw, sw, aw, z, q, hw, th)
def check_inputs(d):
    bad = []
    for k, lo, hi in (("lx", 0, 255), ("fw", 0, W - 1), ("sw", 0, W - 1), ("aw", 0, W - 1), ("z0", 0, 255), ("q0", 0, W - 1), ("hw", 0, 255), ("th", 0, 4095)):
        v = np.asarray(d[k]).astype(np.float64)
        if not (np.min(v) >= lo and np.max(v) <= hi): bad.append("range of " + k)
        elif np.any(v != np.floor(v)): bad.append("whole numbers of " + k)
    for k, hi in (("lx", 15), ("z0", 0), ("hw", 0)):
        v = np.asarray(d[k]).astype(np.float64)[:, 15::16]
        if not np.max(v) <= hi: bad.append("rows 16*g + 15 of " + k)
    return bad
def reference(lx, fw, sw, aw, z0, q0, hw, th):
    x = lx.astype(np.float32).astype(np.int64).reshape(N, 8, 16, W); fd = fw.astype(np.int64).reshape(N, 8, 16, FC)
    sd = sw.astype(np.int64).reshape(N, 8, 16, SC); ad = aw.astype(np.int64).reshape(N, 8, 16, SC)
    z = z0.astype(np.float32).astype(np.int64).reshape(N, 8, 16, T); q = q0.astype(np.int64).reshape(N, 8, T)
    wt = hw.astype(np.int64).reshape(N, 8, 16, 1); lim = th.astype(np.int64).reshape(N, 8, 1); none = np.zeros((N, 8, 1), np.int64)
    own = (np.arange(T)[None, :] & 15) == np.arange(16)[:, None]; BL = T // NB
    for s in range(RO):
        h = hashes(wt, z); col = h >> 2
        stored = np.where(own, q[:, :, None, :], pick(fd, col)); comp = compose(pick(sd, h & (SC - 1)), pick(ad, h >> 3))
        names = np.concatenate([stored, comp], axis=2)
        words = pick(x, names.reshape(N, 8, 32 * T)).reshape(N, 8, 16, 32, T)
        tm = np.sum(np.abs(words[:, :, :15] - z[:, :, :15, None, :]), axis=2) + 16 * (15 - words[:, :, 15])
        bs = np.argmin(tm[:, :, :16], axis=2); bc = 16 + np.argmin(tm[:, :, 16:], axis=2); slow = np.argmax(tm[:, :, :16], axis=2)
        ts, tc = [np.take_along_axis(tm, b[:, :, None, :], 2)[:, :, 0] for b in (bs, bc)]
        cw = tc < ts; win = np.minimum(ts, tc) < lim + none
        wn = np.take_along_axis(names, np.where(cw, bc, bs)[:, :, None, :], 2)[:, :, 0]; ln = np.take_along_axis(names, np.where(cw, bs, bc)[:, :, None, :], 2)[:, :, 0]
        xw = pick(x, wn); top = np.max(words[:, :, :, 16:], axis=3)
        xn = np.array(x); fn = np.array(fd); lo = LN * (s % (T // LN))
        for a in range(N):
            for g in range(8):
                le = np.arange(lo, lo + LN); le = le[win[a, g, le]]
                v = ln[a, g, le]; xn[a, g, 15, v] = np.maximum(x[a, g, 15, v] - 1, 0)
                v, i = np.unique(wn[a, g, le], return_index=True); t = le[i]
                xn[a, g][:15, v] = (x[a, g][:15, v] + z[a, g][:15, t]) >> 1; xn[a, g][15, v] = np.minimum(x[a, g][15, v] + 2, 15)
                le = le[cw[a, g, le]]; c, i = np.unique(col[a, g, le], return_index=True); t = le[i]
                fn[a, g][slow[a, g, t], c] = wn[a, g, t]
        z = np.abs(z - np.where(win[:, :, None, :], xw, top)); z[:, :, 15] = 0
        q = np.where(win, wn, q); none = T - np.sum(win.astype(np.int64), axis=2, keepdims=True); x, fd = xn, fn
        if s < RO - 1:
            z2, q2 = np.zeros_like(z), np.zeros_like(q)
            for a in range(N):
                for b in range(NB):
                    to = (a + 1 + b + s) % N; z2[to, :, :, b * BL:(b + 1) * BL] = z[a, :, :, b * BL:(b + 1) * BL]; q2[to, :, b * BL:(b + 1) * BL] = q[a, :, b * BL:(b + 1) * BL]
            z, q = z2, q2
    return {"yx": x.reshape(N, 128, W).astype(np.float32).astype(BF), "yf": fd.reshape(N, 128, FC).astype(np.float32), "yz": z.reshape(N, 128, T).astype(np.float32).astype(BF), "yq": q.astype(np.float32)}

import numpy as np
from concourse.mybir import AluOpType as A, ActivationFunctionType as F

NS, NBK = 3, 2
MAGIC = 12582912.0
BIG = 67108864.0
bf, f32, i32, u16, f16 = "bfloat16", "float32", "int32", "uint16", "float16"

SCRATCH = {
    "X": ("sbuf", [128, 2112], bf), "FWI": ("sbuf", [128, 512], i32), "FWF": ("sbuf", [128, 576], f32),
    "SWI": ("sbuf", [128, 256], i32), "AWI": ("sbuf", [128, 256], i32), "SWF": ("sbuf", [128, 256], f32), "AWF": ("sbuf", [128, 256], f32),
    "Z": ("sbuf", [128, 768], bf), "D": ("sbuf", [128, 768], f16), "ZS": ("sbuf", [128, 512], bf), "DS": ("sbuf", [128, 512], f16),
    "YZ": ("sbuf", [128, 256], bf), "YQ": ("sbuf", [128, 256], f32), "ZA": ("sbuf", [128, 64], bf),
    "HWI": ("sbuf", [128, 8], i32), "QI": ("sbuf", [128, 256], i32), "THI": ("sbuf", [128, 8], i32), "QF": ("sbuf", [128, 264], f32),
    "ONE": ("sbuf", [128, 144], f32), "EXP": ("sbuf", [128, 128], f32), "SEL": ("sbuf", [128, 144], f32),
    "ID": ("sbuf", [128, 128], bf), "NI": ("sbuf", [128, 128], bf), "E": ("sbuf", [128, 128, 16], bf),
    "BH": ("sbuf", [128, 144], bf), "BT": ("sbuf", [128, 144], bf), "BS": ("sbuf", [128, 144], f16), "BO": ("sbuf", [128, 128], f16),
    "PI": ("sbuf", [128, 8], i32), "CP": ("sbuf", [128, 16], f32), "KN": ("sbuf", [128, 16], f32), "JK": ("sbuf", [128, 32], f32),
    "J32": ("sbuf", [128, 128], bf), "J16": ("sbuf", [128, 128], bf), "TT": ("sbuf", [128, 128], f32),
    "OHS": ("sbuf", [128, 64], bf), "OHC": ("sbuf", [128, 64], bf), "NOH": ("sbuf", [128, 64], bf),
    "R32": ("sbuf", [128, 128], bf), "R16": ("sbuf", [128, 128], bf), "R3M": ("sbuf", [128, 128], bf),
    "RM": ("sbuf", [128, 1024], bf), "RD": ("sbuf", [128, 768], bf),
    "TL": ("sbuf", [128, 32], f32), "TM": ("sbuf", [128, 16], f32), "DUM": ("sbuf", [128, 16], f32), "PB": ("sbuf", [128, 8], f32), "PL": ("sbuf", [128, 8], f32),
    "IOTA": ("sbuf", [128, 2112], f32),
    "SC2": ("sbuf", [128, 128], f32), "SC3": ("sbuf", [128, 128], f32), "LO": ("sbuf", [128, 8], i32), "LP": ("sbuf", [128, 8], i32), "LU": ("sbuf", [128, 8], u16),
    "FL": ("sbuf", [128, 3, 4], f32), "EE": ("sbuf", [128, 3, 4], f32), "M1": ("sbuf", [128, 8], f32), "VV": ("sbuf", [128, 12], f32), "VU": ("sbuf", [128, 12], u16),
    "VR": ("sbuf", [128, 192], f32), "DA": ("sbuf", [128, 768], bf), "DO": ("sbuf", [128, 768], bf),
    "G1": ("sbuf", [128, 12], f32), "G2": ("sbuf", [128, 12], f32), "G3": ("sbuf", [128, 12], f32), "V2": ("sbuf", [128, 12], u16),
    "W1": ("sbuf", [128, 64], f32), "W2": ("sbuf", [128, 64], f32), "W3": ("sbuf", [128, 64], bf), "L3": ("sbuf", [128, 64], bf),
    "F1": ("sbuf", [128, 64], f32), "F2": ("sbuf", [128, 64], f32), "NW": ("sbuf", [128, 8], f32),
    "BOF": ("sbuf", [128, 128], f32), "JL": ("sbuf", [128, 128], f32), "JH": ("sbuf", [128, 128], f16), "X2": ("sbuf", [128, 2112], bf),
    "X1": ("sbuf", [128, 2112], bf), "X3": ("sbuf", [128, 2112], bf),
    "PD0": ("psum", [128, 1024], f32), "PD1": ("psum", [128, 1024], f32), "PK0": ("psum", [128, 512], f32), "PK1": ("psum", [128, 512], f32),
    "PA": ("psum", [128, 512], f32), "PZ": ("psum", [128, 512], f32),
}
for _b in range(NBK):
    SCRATCH.update({
        "UI%d" % _b: ("sbuf", [128, 8], i32), "KI%d" % _b: ("sbuf", [128, 24], i32), "KU%d" % _b: ("sbuf", [128, 24], u16),
        "ZT%d" % _b: ("sbuf", [128, 128], bf), "PG%d" % _b: ("sbuf", [128, 128], f32), "NR%d" % _b: ("sbuf", [128, 128], i32),
        "PR%d" % _b: ("sbuf", [128, 128], i32), "PQ%d" % _b: ("sbuf", [128, 128], i32), "N%d" % _b: ("sbuf", [128, 256], i32), "NU%d" % _b: ("sbuf", [128, 256], u16),
        "WA%d" % _b: ("sbuf", [128, 6240], bf), "DZ%d" % _b: ("sbuf", [128, 128], bf),
        "AB%d" % _b: ("sbuf", [128, 128, 32], bf), "SK%d" % _b: ("sbuf", [128, 256], f32),
        "L%d" % _b: ("sbuf", [128, 2, 8], i32), "I%d" % _b: ("sbuf", [128, 8], i32), "JI%d" % _b: ("sbuf", [128, 2, 8], i32),
        "JU%d" % _b: ("sbuf", [128, 16], u16), "MB%d" % _b: ("sbuf", [128, 4, 128], f16),
    })
DMAS = ["z", "hw", "q", "th", "sw", "aw", "fw", "x", "oz0", "oz1", "oz2", "oq", "ox", "of", "c0", "c1", "c2"]
SEMAPHORES = (["v", "s", "pe", "pl", "snt"] + ["d_" + n for n in DMAS]
              + ["a%s%d%d" % (k, s, b) for k in "zd" for s in range(NS - 1) for b in range(NBK)])
PSUM_KEYS = ("PD0a", "PD1a", "PD0b", "PD1b", "PK0", "PK1", "PA", "PZ")
QPOST, XDB = [0, 0, 1], [1, 1, 1]

CYC, GA, SCA, PEC, FIX, LAT = 1.04, 1.56, 3.8, 0.52, 40.0, 110.0
SEED, TRIES, HEAT = 0, 6000, 400.0
PLAN = []
SHARE = [0, 128] * 6
QS, RS = 3120, 1040


def route(T, topo, s, b, r, kind):
    n = len(T.cores)
    src, dst = T.cores[r], T.cores[(r + 1 + b + s) % n]
    if topo.may_write(src, dst):
        return src, None, dst
    hs = [h for h in topo.cores_of(src) if T.rank_of(h) is None and topo.may_write(h, dst)]
    near = [h for h in hs if topo.die(h) == topo.die(src)] or hs
    return src, (near[0] if kind == "z" else near[-1]), dst


def land(T, kind, s, b):
    c = 256 * (s + 1) + 128 * b
    return (T.Z if kind == "z" else T.D)[:, c:c + 128]


def relay_program(g, core, T, topo):
    sent = 0
    for s in range(NS - 1):
        for b in range(NBK):
            for r in range(len(T.cores)):
                for kind in "zd":
                    src, h, dst = route(T, topo, s, b, r, kind)
                    if h != core:
                        continue
                    n = len(topo.engines(h, dst))
                    sem = T.sem["a%s%d%d" % (kind, s, b)]
                    rid, pid = topo.addr(dst, h)
                    g.wait_ge(sem, n)
                    g.remote_dma(land(T, kind, s, b), land(T, kind, s, b), sem, T.sem.snt, pid, rid, topo.mask(h, dst))
                    sent += n
    if sent:
        g.wait_ge(T.sem.snt, sent)


def build(g, core, T, topo, ops):
    rank = T.rank_of(core)
    last_w, readers = {}, {}

    def op(eng, fn, cost, rd, wr, lat=0.0, sem=None, ext=None):
        me = len(ops)
        deps = set()
        for k in rd:
            if k in last_w:
                deps.add(last_w[k])
            if k in PSUM_KEYS:
                deps.update(o for o in readers.get(k, []) if ops[o]["eng"] != eng)
        for k in wr:
            if k in last_w:
                deps.add(last_w[k])
            deps.update(readers.get(k, []))
        for k in rd:
            readers.setdefault(k, []).append(me)
        for k in wr:
            last_w[k] = me
            readers[k] = []
        deps.discard(me)
        ops.append({"eng": eng, "fn": fn, "cost": cost, "deps": deps, "lat": lat, "sem": sem, "ext": ext, "wr": wr})
        return me

    V, S, PE = g.vector, g.scalar, g.tensor

    def vc(n, c=1.0):
        return FIX + max(64.0, n * c) * CYC

    def gc(n, c=GA):
        return 60.0 + n * c * CYC

    def ts(out, in0, s1, s2, o0, o1, cost, rd, wr):
        if o1 is None:
            return op("v", lambda: V.tensor_scalar(out, in0, s1, None, o0), cost, rd, wr)
        return op("v", lambda: V.tensor_scalar(out, in0, s1, s2, o0, o1), cost, rd, wr)

    def tt(out, in0, in1, o, cost, rd, wr):
        return op("v", lambda: V.tensor_tensor(out, in0, in1, o), cost, rd, wr)

    def cp(out, in_, cost, rd, wr):
        return op("v", lambda: V.tensor_copy(out, in_), cost, rd, wr)

    def ms(ap, c, cost, wr):
        return op("v", lambda: V.memset(ap, c), cost, [], wr)

    def scan(out, d0, d1, o0, o1, cost, rd, wr):
        return op("v", lambda: V.tensor_tensor_scan(out, d0, d1, 0.0, o0, o1), cost, rd, wr)

    def act(out, in_, fn, cost, rd, wr, **kw):
        return op("s", lambda: S.activation(out, in_, fn, **kw), cost, rd, wr)

    def mm(lst, rd, wr, wide=1.0):
        def fn():
            ins = None
            for o, l, r, st, sp, n in lst:
                ins = PE.matmul(o, l, r, st, sp)
            return ins
        return op("pe", fn, sum(max(64, m[5]) for m in lst) * PEC * wide + 60.0, rd, wr)

    def dma(eng, name, out, in_, nbytes, rd, wr, extra=0.0):
        q = g.sync if eng == "sp" else g.scalar
        return op(eng, lambda: q.dma_start(out, in_), 60.0, rd, wr, lat=1800.0 + extra + nbytes / 200.0, sem="d_" + name)

    def pool(fn, n, rd, wr):
        return op("pl", fn, 170.0 + 2 * n * CYC, rd, wr)

    def iota(out, pat, n, key, base=0, cm=0, flt=True):
        if flt:
            return pool(lambda: g.iota(out, pat, base, cm, allow_small_or_imprecise_dtypes=True), n, [], [key])
        return pool(lambda: g.iota(out, pat, base, cm), n, [], [key])

    dma("sp", "z", T.Z[:, 0:256], T.z0[:], 65536, [], ["Z00", "Z01"])
    dma("s", "hw", T.HWI[:, 0:1], T.hw[:], 512, [], ["HWI"])
    dma("s", "q", T.QI[0:8, :], T.q0[:], 8192, [], ["QI"])
    dma("sp", "aw", T.AWI[:], T.aw[:], 131072, [], ["AWI"], 400.0)
    dma("s", "sw", T.SWI[:], T.sw[:], 131072, [], ["SWI"], 1000.0)
    dma("sp", "x", T.X[:, 0:2048], T.lx[:], 524288, [], ["X"], 1700.0)
    dma("s", "fw", T.FWI[:], T.fw[:], 262144, [], ["FWI"], 3000.0)
    dma("sp", "th", T.THI[0:8, 0:1], T.th[:], 32, [], ["THI"], 4000.0)

    CA, C15, CRM, CR2, CWT, CS1, CCAP, CLB, CHW, CA33, CB1, CB2, CTH = [T.CP[:, j:j + 1] for j in range(13)]
    ms(T.ONE[:], 1.0, vc(144), ["ONE"])
    iota(T.PI[:, 0:1], [[1, 1]], 1, "PI0", 0, 1, False)
    pool(lambda: g.affine_select(T.EXP[0:8, :], T.ONE[0:8, 0:128], [[-1, 8], [0, 16]], A.is_equal, 0.0, 0, 1), 128, ["ONE"], ["EXP"])
    pool(lambda: g.affine_select(T.SEL[0:8, :], T.ONE[0:8, :], [[1, 144]], A.is_equal, 0.0, -15, -16), 144, ["ONE"], ["SEL"])
    pool(lambda: g.affine_select(T.ID[:], T.ONE[:, 0:128], [[-1, 128]], A.is_equal, 0.0, 0, 1), 128, ["ONE"], ["ID"])
    iota(T.J16[:], [[0, 8], [1, 16]], 128, "J16")
    iota(T.J32[:], [[0, 4], [1, 32]], 128, "J32")
    iota(T.RM[:], [[0, 64], [256, 16]], 1024, "RM")
    iota(T.TL[:, 0:12], [[0, 3], [16, 4]], 12, "TL", -63)
    iota(T.TL[:, 16:24], [[0, 2], [16, 4]], 8, "TL1", 2048)
    iota(T.TL[:, 24:28], [[16, 4]], 4, "TL2", 512)
    iota(T.PL[:], [[QS, 2], [256, 4]], 8, "PL")
    iota(T.JL[:], [[0, 4], [RS, 2], [1, 16]], 128, "JL")
    iota(T.IOTA[:], [[1, 2112]], 2112, "IOTA")
    ts(T.JH[:], T.JL[:], 0.0625, None, A.mult, None, vc(128), ["JL"], ["JH"])
    for b in range(NBK):
        for j in range(6):
            act(T["WA%d" % b][:, RS * j + 1024:RS * j + RS], T.ONE[:, 0:16], F.Copy, vc(1), ["ONE"], ["WG%d%d" % (b, j)])
    ts(T.PI[:, 4:5], T.PI[:, 0:1], 15, None, A.bitwise_and, None, vc(1), ["PI0"], ["PI4"])
    cp(CA, T.PI[:, 4:5], vc(1), ["PI4"], ["CA"])
    ts(C15, CA, 15.0, None, A.is_equal, None, vc(1), ["CA"], ["C15"])
    for col, key, m, c in ((CRM, "CRM", -1.0, 1.0), (CR2, "CR2", 2.0, 0.0), (CWT, "CWT", -69632.0, 4096.0), (CS1, "CS1", 0.5005, 0.4995),
                           (CCAP, "CCAP", -240.0, 255.0), (CLB, "CLB", -1.0, 0.0)):
        act(col, C15, F.Identity, vc(1), ["C15"], [key], scale=m, bias=c)
    act(CA33, CA, F.Identity, vc(1), ["CA"], ["CA33"], scale=16.0)
    act(CTH, CA, F.Identity, vc(1), ["CA"], ["CTH"], scale=1.0 / 128)
    cp(CHW, T.HWI[:, 0:1], vc(1), ["HWI"], ["CHW"])
    mm([(T.PD0[:, 0:144], T.EXP[0:8, :], T.SEL[0:8, :], True, True, 144), (T.PD0[:, 256:384], T.EXP[0:8, :], T.EXP[0:8, :], True, True, 128)],
       ["EXP", "SEL"], ["PD0a"], 4.0)
    ts(T.BH[:], T.PD0[:, 0:144], CHW, None, A.mult, None, vc(144), ["PD0a", "CHW"], ["BH"])
    cp(T.BS[:], T.PD0[:, 0:144], vc(144), ["PD0a"], ["BS"])
    cp(T.BO[:], T.PD0[:, 256:384], vc(128), ["PD0a"], ["BO"])
    act(T.BT[:], T.PD0[:, 0:144], F.Copy, vc(144), ["PD0a", "CWT"], ["BT"], scale=CWT)
    act(T.BOF[:], T.PD0[:, 256:384], F.Copy, vc(128), ["PD0a"], ["BOF"])
    ts(T.NI[:], T.ID[:], CRM, -1.0, A.mult, A.mult, vc(64), ["ID", "CRM"], ["NI"])
    for i in range(16):
        act(T.E[:, :, i], T.ID[:], F.Copy, vc(128), ["ID"], ["E%d" % i])
    EK = ["E%d" % i for i in range(16)]
    ts(T.TT[:], T.J16[:], CA, -4096.0, A.is_equal, A.mult, vc(128), ["J16", "CA"], ["TT"])
    act(T.TT[:], T.TT[:], F.Identity, vc(128), ["TT"], ["TT"], bias=2048.0)
    cp(T.QF[0:8, 0:256], T.QI[0:8, :], vc(256), ["QI"], ["QF"])
    mm([(T.PD1[:, 0:256], T.EXP[0:8, :], T.QF[0:8, 0:256], True, True, 256)], ["EXP", "QF"], ["PD1a"], 4.0)
    for b in range(NBK):
        tt(T.D[:, 128 * b:128 * b + 128], T.PD1[:, 128 * b:128 * b + 128], T.TT[:], A.add, vc(128), ["PD1a", "TT"], ["D0%d" % b])
    ts(T.SWF[:], T.SWI[:], 1184.0, None, A.add, None, vc(256), ["SWI"], ["SWF"])
    ts(T.AWF[:], T.AWI[:], 32.0, None, A.add, None, vc(256), ["AWI"], ["AWF"])
    ms(T.X[:, 2048:2112], 0.0, vc(32), ["XD"])
    ms(T.FWF[:, 512:576], 0.0, vc(64), ["FD"])
    cp(T.FWF[:, 0:512], T.FWI[:], vc(512), ["FWI"], ["FW"])
    cp(T.QF[0:8, 256:257], T.THI[0:8, 0:1], vc(1), ["THI"], ["QT"])
    mm([(T.PZ[:, 0:1], T.EXP[0:8, :], T.QF[0:8, 256:257], True, True, 1)], ["EXP", "QT"], ["PZ"], 4.0)
    act(T.KN[:, 0:1], T.PZ[:, 0:1], F.Identity, vc(1), ["PZ"], ["KN00"], scale=4096.0, bias=2 * RS + 15 - 4096.0 * 241.0)
    ts(T.KN[:, 1:2], T.KN[:, 0:1], CA, -15.0, A.add, A.add, vc(1), ["KN00", "CA"], ["KN01"])
    act(T.CP[:, 10:12], T.KN[:, 0:2], F.Identity, vc(1), ["KN00", "KN01"], ["CB"], bias=4096.0 * 128)
    ts(T.OHS[:], T.J32[:, 0:64], CA, None, A.is_equal, None, vc(1), ["J32", "CA"], ["OHS"])
    ts(T.OHC[:], T.J32[:, 0:64], -16.0, CA, A.add, A.is_equal, vc(1), ["J32", "CA"], ["OHC"])
    ts(T.NOH[:], T.J32[:, 0:64], CA, 30.0, A.add, A.not_equal, vc(1), ["J32", "CA"], ["NOH"])
    act(T.R32[:], T.J32[:], F.Relu, vc(128), ["J32"], ["R32"], scale=-BIG, bias=BIG)
    act(T.R16[:], T.J16[:], F.Relu, vc(128), ["J16"], ["R16"], scale=-BIG, bias=BIG)
    act(T.R3M[:], T.R32[:], F.Identity, vc(128), ["R32"], ["R3M"], scale=-1.0, bias=2.0)
    pool(lambda: g.affine_select(T.RD[:], T.IOTA[:, 1024:1792], [[0, 12], [1, 64]], A.is_equal, -1.0 / 128, 0, 0), 768, ["IOTA"], ["RD"])
    act(T.PB[:], T.PL[:], F.Identity, vc(1), ["PL", "CA33"], ["PB0"], bias=CA33)
    act(T.TM[:, 0:12], T.TL[:, 0:12], F.Identity, vc(1), ["TL", "CTH"], ["TM"], scale=1.0 / 128, bias=CTH)
    act(T.DUM[:, 0:12], T.TL[:, 16:28], F.Identity, vc(1), ["TL1", "TL2", "CA"], ["DUM"], bias=CA)
    TMK, DUK = ["TM"], ["DUM"]
    act(T.ZA[:], T.Z[:, 0:64], F.Identity, vc(1), ["Z00", "CR2"], ["ZA"], bias=CR2)

    XN = ["X"]
    for s in range(NS):
        XN.append("X%d" % (s + 1) if XDB[s] else XN[-1])

    def zap(s, b, c0=0, c1=128):
        return T.Z[:, 256 * s + 128 * b + c0:256 * s + 128 * b + c1]

    def B(n, b):
        return T["%s%d" % (n, b)]

    def pre(s, b):
        z, zk, k = zap(s, b), "Z%d%d" % (s, b), str(b)
        base = 256 * s + 128 * b
        lst = [(T.PA[:, 0:8], T.BH[:, 15 - a:143 - a], T.Z[:, base + a:base + 128:16], a == 0, a == 15, 8) for a in range(16)]
        lst.append((T.PA[:, 128:256], z, T.NI[:], True, True, 128))
        mm(lst, [zk, "BH", "NI"], ["PA"])
        UI, KI, KU = B("UI", b), B("KI", b), B("KU", b)
        cp(UI[:], T.PA[:, 0:8], vc(8), ["PA"], ["UI" + k])
        act(B("ZT", b)[:], T.PA[:, 128:256], F.Copy, vc(128), ["PA"], ["ZT" + k])
        ts(KI[:, 0:8], UI[:], 2, 511, A.logical_shift_right, A.bitwise_and, vc(8), ["UI" + k], ["KIk" + k])
        ts(KI[:, 8:16], UI[:], 255, None, A.bitwise_and, None, vc(8), ["UI" + k], ["KIs" + k])
        ts(KI[:, 16:24], UI[:], 3, 255, A.logical_shift_right, A.bitwise_and, vc(8), ["UI" + k], ["KIp" + k])
        cp(KU[:], KI[:], vc(24), ["KIk" + k, "KIs" + k, "KIp" + k], ["KU" + k])
        act(B("PG", b)[:], T.AWF[:].indirect(KU[:, 16:24]), F.Copy, gc(128), ["AWF", "KU" + k], ["PG" + k])
        fw, fk = (T.FWI[:], ["FWI"]) if s == 0 else (T.FWF[:, 0:512], ["FW"])
        N, NU = B("N", b), B("NU", b)
        tt(B("NR", b)[:], fw.indirect(KU[:, 0:8]), T.D[:, base:base + 128], A.min, gc(128), fk + ["KU" + k, "D%d%d" % (s, b)], ["NR" + k])
        ts(N[:, 0:128], B("NR", b)[:], 2047, None, A.bitwise_and, None, vc(128), ["NR" + k], ["Ns" + k])
        cp(NU[:, 0:128], N[:, 0:128], vc(128), ["Ns" + k], ["NUs" + k])
        tt(B("PR", b)[:], T.SWF[:].indirect(KU[:, 8:16]), B("PG", b)[:], A.mult, gc(128), ["SWF", "KU" + k, "PG" + k], ["PR" + k])
        ts(B("PQ", b)[:], B("PR", b)[:], 27648, None, A.add, None, vc(128), ["PR" + k], ["PQ" + k])
        ts(N[:, 128:256], B("PQ", b)[:], 5, 2047, A.logical_shift_right, A.bitwise_and, vc(128), ["PQ" + k], ["Nc" + k])
        cp(NU[:, 128:256], N[:, 128:256], vc(128), ["Nc" + k], ["NUc" + k])

    def main(s, b, h):
        k, q = str(b), "%d%d" % (b, h)
        xn = XN[s]
        NU, AB, xw = B("NU", b), B("AB", b), T[xn][:, 0:2048]
        c, WA, x = QS * h, B("WA", b), SHARE[4 * s + 2 * b + h]
        act(WA[:, c:c + 1024], xw.indirect(NU[:, 64 * h:64 * h + 64]), F.Copy, gc(1024), [xn, "NUs" + k], ["WS" + q])
        n0 = 128 + 64 * h
        cp(WA[:, c + RS + x:c + RS + 1024], xw.indirect(NU[:, n0 + x // 16:n0 + 64]), gc(1024 - x), [xn, "NUc" + k], ["WC" + q])
        wck = ["WC" + q]
        if x:
            act(WA[:, c + RS:c + RS + x], xw.indirect(NU[:, n0:n0 + x // 16]), F.Copy, gc(x), [xn, "NUc" + k], ["WD" + q])
            wck.append("WD" + q)
        for r, (wk, pd) in enumerate(((["WS" + q], "PD0"), (wck, "PD1"))):
            for j in range(2):
                o = T[pd][:, 512 * j:512 * j + 512]
                t0 = 64 * h + 32 * j
                mm([(o, B("ZT", b)[:], T.E[:, t0:t0 + 32, :], True, False, 512),
                    (o, T.ID[:], WA[:, c + RS * r + 512 * j:c + RS * r + 512 * j + 512], False, True, 512)],
                   ["ZT" + k, "ID"] + wk + EK, [pd + "ab"[j]])
            act(AB[:, 64 * h:64 * h + 64, 16 * r:16 * r + 16], T[pd][:], F.Abs, vc(1024), [pd + "a", pd + "b"], ["AB%d" % r + q])
        scan(WA[:, c + 2 * RS:c + 2 * RS + 1024], T.RM[:], WA[:, c + RS:c + RS + 1024], A.min, A.max, vc(512), ["RM"] + wck, ["MS" + q])
        pk = "PK%d" % h
        o = T[pk][:, 0:128]
        lst = [(o, T.BO[:], T.JH[:], True, False, 128)]
        lst += [(o, T.BT[:, 15 - a:143 - a], AB[:, 64 * h + a:64 * h + 64:16, :], False, a == 15, 128) for a in range(16)]
        mm(lst, ["BO", "JH", "BT", "AB0" + q, "AB1" + q], [pk])
        scan(B("SK", b)[:, 128 * h:128 * h + 128], T.R32[:], o, A.add, A.min, vc(128), ["R32", pk], ["SC" + q])
        if 2 * b + h == s:
            scan(T.SC2[:], T.R16[:], o, A.add, A.min, vc(128), ["R16", pk], ["SC2"])
            scan(T.SC3[:], T.R3M[:], o, A.add, A.max, vc(128), ["R3M", pk], ["SC3"])

    sent = [0]

    def send(kind, s, b, src_ap, key):
        src, h, dst = route(T, topo, s, b, rank, kind)
        to = dst if h is None else h
        m = topo.mask(src, dst) if h is None else topo.mask(src, h) & topo.mask(h, dst)
        n = bin(m).count("1")
        rid, pid = topo.addr(to, src)
        name = "a%s%d%d" % (kind, s, b)
        sent[0] += n
        op("pl", lambda: g.remote_dma(land(T, kind, s, b), src_ap, T.sem[name], T.sem.snt, pid, rid, m), 400.0, [key],
           [("Z" if kind == "z" else "D") + "%d%d" % (s + 1, b)], lat=2500.0 if h is None else 5000.0, ext=(name, n))

    def post(s, b, hs):
        k = str(b)
        h0, nh = hs[0], len(hs)
        c0, c1, t0, t1, n = 4 * h0, 4 * (h0 + nh), 64 * h0, 64 * (h0 + nh), 64 * nh
        qs = ["%d%d" % (b, h) for h in hs]
        ks = lambda p: [p + q for q in qs]
        WA, L, I, JI, JU, DZ, MB, N = [B(x, b) for x in ("WA", "L", "I", "JI", "JU", "DZ", "MB", "N")]
        sc = B("SK", b)[:, 32 * c0 + 31:32 * c1:32]
        for j in range(2):
            ts(L[:, j, c0:c1], sc, T.KN[:, 2 * s + j:2 * s + j + 1], None, A.min, None, vc(8), ks("SC") + ["KN%d%d" % (s, j)], ks("L%d" % j))
        ts(I[:, c0:c1], L[:, 0, c0:c1], 4095, None, A.bitwise_and, None, vc(8), ks("L0"), ks("I"))
        ts(JI[:, 1, c0:c1], L[:, 1, c0:c1], 63, None, A.bitwise_and, None, vc(8), ks("L1"), ks("JJ"))
        tt(JI[:, 0, c0:c1], I[:, c0:c1], T.PB[:, 0:c1 - c0], A.add, vc(16), ks("I") + ["PB0"], ks("JI"))
        u0, w = 2 * c0, c1 - c0
        cp(JU[:, u0:u0 + 2 * w], JI[:, :, c0:c1], vc(8), ks("JI") + ks("JJ"), ks("JU"))
        JA, JB = JU[:, u0:u0 + w], JU[:, u0 + w:u0 + 2 * w]
        wk = ks("WS") + ks("WC") + ks("WD") + ks("MS") + ks("JU") + ["WG%d%d" % (b, j) for j in range(6)] + ["Z%d%d" % (s, b)]
        tt(DZ[:, t0:t1], WA[:, QS * h0:QS * (h0 + nh)].indirect(JA), zap(s, b, t0, t1), A.subtract, gc(n), wk, ks("DZ"))
        lastst = s == NS - 1
        if lastst:
            act(T.YZ[:, 128 * b + t0:128 * b + t1], DZ[:, t0:t1], F.Abs, vc(n), ks("DZ") + ["CRM"], ks("YZ"), scale=CRM)
            dma("sp", "oz%d" % (b + h0), T.yz[:, 128 * b + t0:128 * b + t1], T.YZ[:, 128 * b + t0:128 * b + t1], 256 * n, ks("YZ"), [])
        tt(MB[:, 0, t0:t1], T.OHS[:].indirect(JB), N[:, t0:t1], A.mult, gc(n), ["OHS", "Ns" + k] + ks("JU"), ks("MB0"))
        tt(MB[:, 2, t0:t1], T.OHC[:].indirect(JB), N[:, 128 + t0:128 + t1], A.mult, gc(n), ["OHC", "Nc" + k] + ks("JU"), ks("MB2"))
        if lastst:
            o = T.PZ[0:8, 128:128 + n]
            mm([(o, T.BO[:, 0:128:16], MB[:, 0, t0:t1], True, False, n), (o, T.BO[:, 0:128:16], MB[:, 2, t0:t1], False, True, n)],
               ["BO"] + ks("MB0") + ks("MB2"), ["PZ"])
            act(T.YQ[0:8, 128 * b + t0:128 * b + t1], o, F.Copy, vc(n), ["PZ"], ks("YQ"))

    def leave(s, b):
        k, MB = str(b), B("MB", b)
        ks = lambda p: [p + k + "0", p + k + "1"]
        zs = T.ZS[:, 256 * s + 128 * b:256 * s + 128 * b + 128]
        act(zs, B("DZ", b)[:], F.Abs, vc(128), ks("DZ") + ["CRM", "CR2"], ["ZS%d%d" % (s, b)], scale=CRM, bias=CR2)
        send("z", s, b, zs, "ZS%d%d" % (s, b))
        o = T.PZ[:, 128:256]
        mm([(o, T.BO[:], MB[:, 0, :], True, False, 128), (o, T.BO[:], MB[:, 2, :], False, True, 128)], ["BO"] + ks("MB0") + ks("MB2"), ["PZ"])
        ds = T.DS[:, 256 * s + 128 * b:256 * s + 128 * b + 128]
        tt(ds, o, T.TT[:], A.add, vc(128), ["PZ", "TT"], ["DS%d%d" % (s, b)])
        send("d", s, b, ds, "DS%d%d" % (s, b))
        act(T.JK[:, 8 * b:8 * b + 8], B("SK", b)[:, 31:256:32], F.Sign, vc(8), ks("SC") + ["KN%d0" % s], ["JK" + k, "NW" + k],
            bias=T.KN[:, 2 * s:2 * s + 1], scale=-1.0, accum_out=T.NW[:, b:b + 1])

    def count(s):
        o = T.PZ[:, 256:257]
        mm([(o, T.BOF[:], T.NW[:, b:b + 1], b == 0, b == 1, 1) for b in range(NBK)], ["BOF", "NW0", "NW1"], ["PZ"], 4.0)
        for j in range(2):
            act(T.KN[:, 2 * s + 2 + j:2 * s + 3 + j], o, F.Identity, vc(1), ["PZ", "CB"], ["KN%d%d" % (s + 1, j)],
                bias=T.CP[:, 10 + j:11 + j], scale=-2048.0)

    def learn_a(s):
        b, h = s // 2, s % 2
        k, q = str(b), "%d%d" % (b, h)
        c0, t0 = 4 * h, 64 * h
        L, I, MB, N, KI = [B(x, b) for x in ("L", "I", "MB", "N", "KI")]
        tt(T.LO[:, 0:4], T.SC2[:, 15:128:32], T.SC2[:, 31:128:32], A.max, vc(8), ["SC2"], ["LO0"])
        cp(T.LO[:, 4:8], T.SC3[:, 15:128:32], vc(8), ["SC3"], ["LO1"])
        ts(T.LP[:], T.LO[:], 63, None, A.bitwise_and, None, vc(8), ["LO0", "LO1"], ["LP"])
        cp(T.LU[:], T.LP[:], vc(8), ["LP"], ["LU"])
        tt(MB[:, 1, t0:t0 + 64], T.OHS[:].indirect(T.LU[:, 0:4]), N[:, t0:t0 + 64], A.mult, gc(64), ["OHS", "Ns" + k, "LU"], ["MB1"])
        tt(MB[:, 3, t0:t0 + 64], T.OHC[:].indirect(T.LU[:, 0:4]), N[:, 128 + t0:192 + t0], A.mult, gc(64), ["OHC", "Nc" + k, "LU"], ["MB3"])
        ts(T.FL[:, 0:2, :], L[:, :, c0:c0 + 4], T.KN[:, 2 * s + 1:2 * s + 2], None, A.is_ge, None, vc(8), ["L0" + q, "L1" + q, "KN%d1" % s], ["FL0"])
        tt(T.FL[:, 2, :], T.SC2[:, 31:128:32], L[:, 0, c0:c0 + 4], A.not_equal, vc(8), ["SC2", "L0" + q], ["FL1"])
        tt(T.EE[:], T.FL[:], T.DUM[:, 0:12], A.mult, vc(24), ["FL0", "FL1"] + DUK, ["EE"])
        mm([(T.PZ[:, 288:304], T.BS[:, 15 - a:143 - a], MB[:, :, t0 + a:t0 + 64:16], a == 0, a == 15, 16) for a in range(16)],
           ["BS", "MB0" + q, "MB2" + q, "MB1", "MB3"], ["PZ"])
        tt(T.M1[:], T.PZ[:, 288:296], T.EE[:, 0:2, :], A.max, vc(8), ["PZ", "EE"], ["M1"])
        tt(T.VV[:, 0:8], T.PZ[:, 296:304], T.M1[:], A.max, vc(8), ["PZ", "M1"], ["VV0"])
        tt(T.VV[:, 8:12], KI[:, c0:c0 + 4], T.EE[:, 2, :], A.max, vc(8), ["KIk" + k, "EE"], ["VV1"])
        cp(T.VU[:], T.VV[:], vc(12), ["VV0", "VV1"], ["VU"])
        act(T.VR[:], T.IOTA[:].indirect(T.VU[:]), F.Copy, gc(192), ["IOTA", "VU"], ["VR"])
        for j in range(12):
            act(T.DA[:, 64 * j:64 * j + 64], T.VR[:, 64 * (j // 4):64 * (j // 4) + 64], F.Abs, vc(64), ["VR", "VV0", "VV1"], ["DA%d" % j],
                bias=T.VV[:, j:j + 1], scale=-1.0)
        scan(T.DO[:], T.RD[:], T.DA[:], A.add, A.min, vc(384), ["RD"] + ["DA%d" % j for j in range(12)], ["DO"])
        tt(T.G1[:], T.DO[:, 63:768:64], T.TM[:, 0:12], A.not_equal, vc(24), ["DO"] + TMK, ["G1"])
        tt(T.G2[:], T.G1[:], T.DUM[:, 0:12], A.mult, vc(24), ["G1"] + DUK, ["G2"])
        tt(T.G3[:], T.G2[:], T.VV[:], A.max, vc(24), ["G2", "VV0", "VV1"], ["G3"])
        cp(T.V2[:], T.G3[:], vc(12), ["G3"], ["V2"])
        za, zk = (T.ZA[:], "ZA") if s == 0 else (zap(s, b, t0, t0 + 64), "Z%d%d" % (s, b))
        xn = XN[s]
        tt(T.W1[:], T[xn][:].indirect(T.VU[:, 0:4]), za, A.add, gc(64), [xn, xn + "D", "VU", zk], ["W1"])
        ts(T.W2[:], T.W1[:], CS1, MAGIC, A.mult, A.add, vc(64), ["W1", "CS1"], ["W2"])
        ts(T.W3[:], T.W2[:], -MAGIC, CCAP, A.add, A.min, vc(64), ["W2", "CCAP"], ["W3"])
        act(T.L3[:], T[xn][:].indirect(T.VU[:, 4:8]), F.Relu, gc(64), [xn, xn + "D", "VU", "CLB"], ["L3"], bias=CLB)
        tt(T.F1[:], T.FWF[:].indirect(T.VU[:, 8:12]), T.VR[:, 0:64], A.subtract, gc(64), ["FW", "FD", "VU", "VR"], ["F1"])
        tt(T.F2[:], T.NOH[:].indirect(T.LU[:, 4:8]), T.F1[:], A.mult, gc(64), ["NOH", "LU", "F1"], ["F2"])

    def learn_b(s):
        tt(T.FWF[:].indirect(T.V2[:, 8:12]), T.F2[:], T.VR[:, 0:64], A.add, gc(64, SCA), ["F2", "VR", "V2"], ["FW", "FD"])
        xn = XN[s + 1]
        xo, xk = T[xn], [xn, xn + "D"]
        cp(xo[:].indirect(T.V2[:, 4:8]), T.L3[:], gc(64, SCA), ["L3", "V2"], xk)
        cp(xo[:].indirect(T.V2[:, 0:4]), T.W3[:], gc(64, SCA), ["W3", "V2"], xk)

    for s in range(NS):
        for b in range(NBK):
            pre(s, b)
            if b == 1 and XN[s + 1] != XN[s]:
                xa, xb = XN[s], XN[s + 1]
                dma("sp", "c%d" % s, T[xb][:], T[xa][:], 540672, [xa, xa + "D", "D%d1" % s], [xb, xb + "D"])
            first = s % 2 if b == s // 2 else 0
            main(s, b, first)
            if b == s // 2 and QPOST[s]:
                post(s, b, [first])
                learn_a(s)
                main(s, b, 1 - first)
                post(s, b, [1 - first])
            else:
                main(s, b, 1 - first)
                post(s, b, [0, 1])
                if b == s // 2:
                    learn_a(s)
            if s < NS - 1:
                leave(s, b)
        learn_b(s)
        if s < NS - 1:
            count(s)
    dma("sp", "of", T.yf[:], T.FWF[:, 0:512], 262144, ["FW"], [])
    dma("sp", "ox", T.yx[:], T[XN[NS]][:, 0:2048], 524288, [XN[NS]], [], 500.0)
    dma("sp", "oq", T.yq[:], T.YQ[0:8, :], 8192, ["YQ00", "YQ01", "YQ10", "YQ11"], [])
    return sent[0]


def schedule(ops):
    n = len(ops)
    succ = [[] for _ in range(n)]
    for i, o in enumerate(ops):
        for d in o["deps"]:
            succ[d].append(i)
    pred = [sorted(o["deps"]) for o in ops]
    names = sorted(set(o["eng"] for o in ops))
    eng = [names.index(o["eng"]) for o in ops]
    cost = [o["cost"] for o in ops]
    lat = [o["lat"] + LAT for o in ops]
    big = 1e18

    def place(key, before, after, fwd):
        left = [len(b) for b in before]
        k = np.array([key[i] if not left[i] else big for i in range(n)])
        fin, st, end = [0.0] * n, [0.0] * n, 0.0
        S, E = [[] for _ in names], [[] for _ in names]
        for _ in range(n):
            i = int(k.argmin())
            k[i] = big
            c, t = cost[i], 0.0
            for d in before[i]:
                if fin[d] > t:
                    t = fin[d]
            if not fwd:
                t += lat[i]
            s, e = S[eng[i]], E[eng[i]]
            lo, hi = 0, len(e)
            while lo < hi:
                mid = (lo + hi) // 2
                if e[mid] <= t:
                    lo = mid + 1
                else:
                    hi = mid
            m = len(s)
            while lo < m and s[lo] < t + c:
                if e[lo] > t:
                    t = e[lo]
                lo += 1
            s.insert(lo, t)
            e.insert(lo, t + c)
            st[i] = t
            fin[i] = t + c + (lat[i] if fwd else 0.0)
            if fin[i] > end:
                end = fin[i]
            for j in after[i]:
                left[j] -= 1
                if not left[j]:
                    k[j] = key[j]
        return st, end

    def there_and_back(key, rounds):
        best = None
        for r in range(rounds):
            st, end = place(key, pred, succ, True)
            if best is None or end < best[1]:
                best = (st, end)
            if r + 1 < rounds:
                sb, _ = place([-(st[i] + cost[i] + lat[i]) for i in range(n)], succ, pred, False)
                key = [-(sb[i] + cost[i]) for i in range(n)]
        return best

    prio = [0.0] * n
    for i in range(n - 1, -1, -1):
        prio[i] = cost[i] + lat[i] + max([prio[j] for j in succ[i]] + [0.0])
    st, end = there_and_back([-p for p in prio], 8)
    rng = np.random.default_rng(SEED)
    cur, cend = st, end
    for it in range(TRIES):
        a = np.array(cur)
        mid, kind = rng.random() * cend, it % 4
        if kind == 0:
            key = a + rng.standard_normal(n) * 300.0
        elif kind == 1:
            key = a + rng.standard_normal(n) * 1200.0 * (np.abs(a - mid) < 5000.0)
        else:
            i, d = int(rng.integers(n)), rng.random() * 4000.0
            nb, sg = (pred, -1.0) if kind == 2 else (succ, 1.0)
            key, todo, seen = a.copy(), [i], {i}
            while todo:
                j = todo.pop()
                key[j] += sg * d
                for m in nb[j]:
                    if m not in seen and abs(a[m] - a[i]) < d:
                        seen.add(m)
                        todo.append(m)
        s2, e2 = there_and_back(key.tolist(), 2 if it % 3 else 1)
        if e2 <= cend + HEAT * (1.0 - it / TRIES) * rng.random():
            cur, cend = s2, e2
            if e2 < end:
                st, end = s2, e2
    for i in range(n):
        ops[i]["t"] = st[i]
    return sorted(range(n), key=lambda i: (st[i], i)), end


def rank_program(g, core, T, topo):
    if T.rank_of(core) is None:
        relay_program(g, core, T, topo)
        return
    ops = []
    sent = build(g, core, T, topo, ops)
    if not PLAN:
        PLAN.append(schedule(ops)[0])
    order = PLAN[0]
    queue = {"v": g.vector, "s": g.scalar, "pe": g.tensor, "pl": g, "sp": g.sync}
    cnt, waited, tok, final = {}, {}, {}, {}
    for i in order:
        o = ops[i]
        e = o["eng"]
        need = {}
        for d in o["deps"]:
            sm, v = tok[d]
            need[sm] = max(need.get(sm, 0), v)
        for sm in sorted(need):
            if waited.get((e, sm), 0) < need[sm]:
                queue[e].wait_ge(T.sem[sm], need[sm])
                waited[(e, sm)] = need[sm]
        ins = o["fn"]()
        if o["ext"] is not None:
            tok[i] = o["ext"]
        elif o["sem"] is not None:
            ins.then_inc(T.sem[o["sem"]], 16)
            tok[i] = (o["sem"], 16)
        else:
            cnt[e] = cnt.get(e, 0) + 1
            ins.then_inc(T.sem[e], 1)
            tok[i] = (e, cnt[e])
        final[tok[i][0]] = tok[i][1]
    final["snt"] = sent
    for sm in sorted(final):
        g.wait_ge(T.sem[sm], final[sm])
